import numpy as np
import ml_dtypes


def mxq(x, axis, fmt="e4m3"):
    dtype, down = {"e4m3": (ml_dtypes.float8_e4m3fn, 7), "e5m2": (ml_dtypes.float8_e5m2, 14)}[fmt]
    v = np.moveaxis(np.asarray(x, np.float32).astype(ml_dtypes.bfloat16).astype(np.float64), axis, -1)
    blocks = v.reshape(v.shape[:-1] + (-1, 32))
    amax = np.abs(blocks).max(-1, keepdims=True)
    byte = np.maximum(np.where(amax > 0, np.frexp(amax)[1] - 1 + 127, 0) - down, 1)
    scale = np.exp2(byte - 127.0)
    codes = (blocks / scale).astype(np.float32).astype(dtype).astype(np.float64)
    return np.moveaxis((codes * scale).reshape(v.shape), -1, axis)


WIDE = False


def mx_kscale(k):
    if not WIDE:
        return np.ones(k)
    levels = np.array([10, -10, 5, -5, 0])
    if k % 512:
        return np.exp2(np.random.permutation(np.resize(levels, k // 32))).repeat(32)
    a = np.empty((k // 512, 16))
    for p in range(k // 512):
        a[p, :8] = np.random.permutation(np.resize(levels, 8))
        for g in range(8):
            far = levels[np.abs(levels - a[p, g]) >= 10]
            a[p, g + 8] = far[np.random.randint(len(far))]
    return np.exp2(a.ravel()).repeat(32)


def f64(x):
    return np.asarray(x).astype(np.float64)


def striped8(idx):
    return np.asarray(idx).reshape(8, -1, 16).transpose(0, 2, 1).reshape(128, -1).astype(np.uint16)


def unstriped8(offs):
    return offs.reshape(8, 16, -1).transpose(0, 2, 1).reshape(8, -1).astype(np.int64)


def pick8(x, idx, run):
    r = np.arange(len(x))
    return x[r[:, None], idx[r % (8 * run) // run]]


E2M1 = np.array([0.0, 0.5, 1.0, 1.5, 2.0, 3.0, 4.0, 6.0, -0.0, -0.5, -1.0, -1.5, -2.0, -3.0, -4.0, -6.0])


def pack_weight(w, fmt):
    k, n = w.shape
    w = f64(np.asarray(w, np.float32).astype(ml_dtypes.bfloat16)).reshape(k // 32, 32, n)
    amax = np.abs(w).max(1)
    if fmt == "e4m3":
        byte = np.frexp(amax)[1] - 1 + 127 - 7
    else:
        mant, ex = np.frexp(amax / 6.0)
        byte = np.where(mant > 0.5, ex, ex - 1) + 127
    byte = np.clip(np.where(amax > 0, byte, 1), 1, 254)
    scaled = (w * np.exp2(127.0 - byte)[:, None, :]).reshape(k, n).astype(np.float32)
    by_word = np.ascontiguousarray(scaled.reshape(k // 512, 128, 4, n).transpose(0, 1, 3, 2))
    if fmt == "e4m3":
        words = by_word.astype(ml_dtypes.float8_e4m3fn).view(np.uint8)
    else:
        c = by_word.astype(ml_dtypes.float4_e2m1fn).view(np.uint8) & 0xF
        words = (c[..., 0::2] | (c[..., 1::2] << 4)).reshape(k // 512, 128, 2 * n)
    return np.ascontiguousarray(words), np.ascontiguousarray(byte.astype(np.uint8).reshape(k // 512, 16, n))


def unpack_weight(words, scales, fmt):
    g, _, n = scales.shape
    words = np.ascontiguousarray(words).reshape(g, 128, n, -1)
    if fmt == "e4m3":
        vals = words.view(ml_dtypes.float8_e4m3fn).astype(np.float64)
    else:
        nib = np.empty((g, 128, n, 4), np.uint8)
        nib[..., 0::2] = words & 0xF
        nib[..., 1::2] = words >> 4
        vals = E2M1[nib]
    vals = vals * np.repeat(np.exp2(scales.astype(np.float64) - 127.0), 8, axis=1)[..., None]
    return vals.transpose(0, 1, 3, 2).reshape(g * 512, n)


D, T, U, Z, I, Q, E = 512, 1024, 1024, 1024, 512, 512, 256


def setup_inputs():
    n = np.random.standard_normal
    idx = np.stack([np.random.permutation(T)[:I] for _ in range(8)])
    idx2 = np.stack([np.random.permutation(U)[:I] for _ in range(8)])
    idx3 = np.stack([np.random.permutation(Z)[:I] for _ in range(8)])
    idx4 = np.stack([np.random.permutation(Z)[:I] for _ in range(8)])
    idx5 = np.stack([np.random.permutation(Z)[:I] for _ in range(8)])
    idx6 = np.stack([np.random.permutation(Z)[:I] for _ in range(8)])
    fd = mx_kscale(D)
    fq = mx_kscale(Q)
    keysp = pack_weight(n((D, T)) / fd[:, None], "e2m1")
    notesp = pack_weight(n((D, U)) / fd[:, None], "e4m3")
    mixp = pack_weight(n((Q, E)) * 1.0 / np.sqrt(Q) / fq[:, None], "e4m3")
    return {
        "query": (n((D, Q)) * 1.0 / np.sqrt(D) * fd[:, None]).astype(np.float32),
        "query2": (n((D, Q)) * 1.0 / np.sqrt(D) * fd[:, None]).astype(np.float32),
        "keys_words": keysp[0],
        "keys_scales": keysp[1],
        "notes_words": notesp[0],
        "notes_scales": notesp[1],
        "rowf": (np.random.uniform(0.5, 2.0, (Q, 1)) * fq[:, None]).astype(np.float32),
        "mix_words": mixp[0],
        "mix_scales": mixp[1],
        "offs": striped8(idx),
        "offs2": striped8(idx2),
        "offs3": striped8(idx3),
        "offs4": striped8(idx4),
        "offs5": striped8(idx5),
        "offs6": striped8(idx6),
    }


def reference(query, query2, keys_words, keys_scales, notes_words, notes_scales, rowf, mix_words, mix_scales, offs, offs2, offs3, offs4, offs5, offs6):
    idx = unstriped8(offs)
    idx2 = unstriped8(offs2)
    idx3 = unstriped8(offs3)
    idx4 = unstriped8(offs4)
    idx5 = unstriped8(offs5)
    idx6 = unstriped8(offs6)
    keysu = unpack_weight(keys_words, keys_scales, "e2m1")
    notesu = unpack_weight(notes_words, notes_scales, "e4m3")
    mixu = unpack_weight(mix_words, mix_scales, "e4m3")
    queryq = mxq(f64(query), 0, "e4m3")
    a = queryq.T @ keysu
    query2q = mxq(f64(query2), 0, "e4m3")
    b = query2q.T @ notesu
    w = pick8(a, idx, 64) + pick8(b, idx2, 64)
    f1 = np.zeros((Q, Z))
    f1[np.arange(Q)[:, None], idx3[np.arange(Q) % 512 // 64]] = w
    v = pick8(f1, idx4, 64) - w
    f2 = np.zeros((Q, Z))
    f2[np.arange(Q)[:, None], idx5[np.arange(Q) % 512 // 64]] = v
    cc = f1 - f2
    g = pick8(cc, idx6, 64) + w
    gw = g * f64(rowf)
    gwq = mxq(gw, 0, "e4m3")
    y = mixu.T @ gwq
    return y

@@ -1,0 +1,237 @@
+from contextlib import ExitStack
+
+import concourse.mybir as mybir
+
+D, T, Z, I, Q, E = 512, 1024, 1024, 512, 512, 256
+FLOPS = 2 * D * Q * T * 2 + 2 * Q * E * I
+
+F32 = mybir.dt.float32
+BF16 = mybir.dt.bfloat16
+I32 = mybir.dt.int32
+U32 = mybir.dt.uint32
+U16 = mybir.dt.uint16
+U8 = mybir.dt.uint8
+FP8X4 = mybir.dt.float8_e4m3fn_x4
+FP4X4 = mybir.dt.float4_e2m1fn_x4
+ADD = mybir.AluOpType.add
+SUB = mybir.AluOpType.subtract
+MUL = mybir.AluOpType.mult
+COPY = mybir.ActivationFunctionType.Copy
+
+P = 128
+PACK = 4
+BANK = 512
+HALF = I // 2
+
+
+def tile_attend_auction_twoq_mixed_kernel(tc, query, query2, keys_words, keys_scales, notes_words, notes_scales,
+                                           rowf, mix_words, mix_scales, offs, offs2, offs3, offs4, offs5, offs6, out):
+    nc = tc.nc
+    with ExitStack() as ctx:
+        sb = ctx.enter_context(tc.tile_pool(name="sb", bufs=1))
+        ps = ctx.enter_context(tc.psum_pool(name="ps", bufs=4))
+
+        def tile(shape, dtype, name, tag=None):
+            return sb.tile(shape, dtype, name=name, tag=tag or name, align_bytes=64)
+
+        def load_list(src, name):
+            lst = sb.tile([P, I // 16], U16, name=name)
+            nc.sync.dma_start(lst[:], src)
+            return lst
+
+        def zeroed_plane(width, name):
+            plane = tile([P, width], U8, name)
+            nc.vector.memset(plane[:].bitcast(U32), 0)
+            return plane
+
+        def load_plane(engine, plane, scales):
+            rows = scales[0].bitcast(I32).rearrange("(b f) c -> f b c", f=4)
+            for f in range(4):
+                engine.dma_start(out=plane[f:P:32, :].bitcast(I32), in_=rows[f])
+
+        def load_query(src, name):
+            rows = src.rearrange("(p j) q -> p j q", j=PACK)
+            halves = []
+            for u in range(2):
+                raw = tile([P, 2, Q], F32, name + "_raw%d" % u)
+                nc.sync.dma_start(out=raw[:], in_=rows[:, 2 * u:2 * u + 2, :])
+                halves.append(raw)
+            return halves
+
+        def cast_query(halves, name):
+            grouped = tile([P, Q * PACK], BF16, name + "_bf")
+            dst = grouped[:].rearrange("p (r m j) -> p m r j", r=PACK, j=PACK)
+            for u in range(2):
+                nc.vector.tensor_copy(out=dst[:, :, :, 2 * u:2 * u + 2],
+                                      in_=halves[u][:].rearrange("p j (m r) -> p m r j", r=PACK))
+            codes = tile([P, Q], U32, name + "_codes")
+            plane = tile([P, Q], U8, name + "_plane")
+            for lo, hi in ((0, P), (P, 2 * P), (2 * P, 4 * P)):
+                nc.vector.quantize_mx(out=codes[:, lo:hi].bitcast(FP8X4), scales=plane[:, lo:hi],
+                                      in_=grouped[:, PACK * lo:PACK * hi])
+            return codes, plane
+
+        notes_plane = zeroed_plane(T, "notes_plane")
+        keys_plane = zeroed_plane(T, "keys_plane")
+        lst2 = load_list(offs2, "lst2")
+        load_plane(nc.scalar, notes_plane, notes_scales)
+        q2_raw = load_query(query2, "q2")
+        notes = tile([P, T], I32, "notes")
+        nc.sync.dma_start(out=notes[:], in_=notes_words[0].rearrange("p n t -> p (n t)").bitcast(I32))
+        load_plane(nc.scalar, keys_plane, keys_scales)
+        q1_raw = load_query(query, "q1")
+        keys = tile([P, 2 * T], U8, "keys")
+        nc.sync.dma_start(out=keys[:].bitcast(I32), in_=keys_words[0].bitcast(I32))
+        lst1 = load_list(offs, "lst1")
+        lst3 = load_list(offs3, "lst3")
+        lst4 = load_list(offs4, "lst4")
+        lst5 = load_list(offs5, "lst5")
+        lst6 = load_list(offs6, "lst6")
+        factor = tile([P, PACK], F32, "factor")
+        nc.sync.dma_start(out=factor[:], in_=rowf.rearrange("(p r) o -> p (r o)", r=PACK))
+        mix = tile([P, E], I32, "mix")
+        nc.sync.dma_start(out=mix[:], in_=mix_words[0].rearrange("p n t -> p (n t)").bitcast(I32))
+
+        q2_codes, q2_plane = cast_query(q2_raw, "q2")
+        q1_codes, q1_plane = cast_query(q1_raw, "q1")
+
+        a = [tile([P, T], F32, "a%d" % r) for r in range(PACK)]
+        b = [tile([P, T], F32, "b%d" % r) for r in range(2)]
+        b += [tile([P, T], F32, "b%d" % r, tag="a%d" % (r - 2)) for r in range(2, PACK)]
+        f1 = [tile([P, Z], F32, "f1_0"), tile([P, Z], F32, "f1_1"), tile([P, Z], F32, "f1_2", tag="b1")]
+        f2 = [tile([P, Z], F32, "f2_0", tag="q1_bf"), tile([P, Z], F32, "f2_1", tag="a2")]
+        cc = [tile([P, Z], F32, "cc%d" % r) for r in range(PACK)]
+        ga = [tile([P, I], F32, "ga%d" % r) for r in range(PACK)]
+        gb = [tile([P, I], F32, "gb%d" % r) for r in range(PACK)]
+        w = [tile([P, I], F32, "w%d" % r) for r in range(PACK)]
+        gf = [tile([P, I], F32, "gf%d" % r) for r in range(PACK)]
+        v = [tile([P, I], F32, "v%d" % r) for r in range(PACK)]
+        gc = [tile([P, I], F32, "gc%d" % r) for r in range(PACK)]
+        g = [tile([P, I], F32, "g%d" % r) for r in range(PACK)]
+        gw = tile([P, PACK, I], BF16, "gw")
+
+        def scores_b(r):
+            rows = slice(r * P, (r + 1) * P)
+            for h in range(2):
+                cols = slice(h * BANK, (h + 1) * BANK)
+                bank = ps.tile([P, BANK], F32, name="bank_b")
+                nc.tensor.matmul_mx(out=bank[:], lhsT=q2_codes[:, rows].bitcast(FP8X4), lhsT_scale=q2_plane[:, rows],
+                                    rhs=notes[:, cols].bitcast(FP8X4), rhs_scale=notes_plane[:, cols],
+                                    start=True, stop=True)
+                nc.scalar.activation(b[r][:, cols], bank[:], COPY)
+
+        def scores_a(r):
+            rows = slice(r * P, (r + 1) * P)
+            for h in range(2):
+                cols = slice(h * BANK, (h + 1) * BANK)
+                bank = ps.tile([P, BANK], F32, name="bank_a")
+                nc.tensor.matmul_mx(out=bank[:], lhsT=q1_codes[:, rows].bitcast(FP8X4), lhsT_scale=q1_plane[:, rows],
+                                    rhs=keys[:, 2 * h * BANK:2 * (h + 1) * BANK].bitcast(FP4X4),
+                                    rhs_scale=keys_plane[:, cols], start=True, stop=True)
+                if r == 0 and h == 0:
+                    nc.vector.tensor_copy(a[r][:, cols], bank[:])
+                else:
+                    nc.scalar.activation(a[r][:, cols], bank[:], COPY)
+
+        def gather_b(r):
+            nc.scalar.activation(gb[r][:], b[r][:].indirect(lst2[:]), COPY)
+
+        def bids(r):
+            nc.scalar.activation(ga[r][:], a[r][:].indirect(lst1[:]), COPY)
+            nc.gpsimd.tensor_tensor(w[r][:], ga[r][:], gb[r][:], ADD)
+
+        def place_w(r):
+            nc.vector.tensor_copy(f1[r % 3][:].indirect(lst3[:]), w[r][:])
+
+        def rival(r):
+            nc.scalar.activation(gf[r][:], f1[r % 3][:].indirect(lst4[:]), COPY)
+            nc.gpsimd.tensor_tensor(v[r][:], gf[r][:], w[r][:], SUB)
+
+        def place_v(r):
+            nc.vector.tensor_copy(f2[r % 2][:].indirect(lst5[:]), v[r][:])
+
+        def difference(r, engine):
+            engine.tensor_tensor(cc[r][:], f1[r % 3][:], f2[r % 2][:], SUB)
+
+        def gather_cc(r, lo, hi):
+            nc.scalar.activation(gc[r][:, lo:hi], cc[r][:].indirect(lst6[:, lo // 16:hi // 16]), COPY)
+
+        def result(r, lo, hi, engine):
+            engine.tensor_tensor(g[r][:, lo:hi], gc[r][:, lo:hi], w[r][:, lo:hi], ADD)
+
+        def weigh(r, lo, hi, engine):
+            engine.tensor_scalar(gw[:, r, lo:hi], g[r][:, lo:hi], factor[:, r:r + 1], 0.0, MUL, ADD)
+
+        nc.vector.memset(f1[0][:], 0.0)
+        nc.vector.memset(f1[1][:], 0.0)
+        mix_plane = zeroed_plane(E, "mix_plane")
+        load_plane(nc.sync, mix_plane, mix_scales)
+        scores_b(0)
+        gather_b(0)
+        scores_b(1)
+        scores_a(0)
+        nc.vector.tensor_tensor(w[0][:], a[0][:].indirect(lst1[:]), gb[0][:], ADD)
+        place_w(0)
+        nc.gpsimd.memset(f2[0][:], 0.0)
+        gather_b(1)
+        nc.gpsimd.memset(f1[2][:], 0.0)
+        scores_a(1)
+        bids(1)
+        place_w(1)
+        scores_b(2)
+        rival(0)
+        place_v(0)
+        scores_a(2)
+        gather_b(2)
+        bids(2)
+        nc.gpsimd.memset(f2[1][:], 0.0)
+        place_w(2)
+        rival(1)
+        place_v(1)
+        difference(0, nc.gpsimd)
+        scores_b(3)
+        scores_a(3)
+        gather_b(3)
+        bids(3)
+        place_w(3)
+        rival(2)
+        place_v(2)
+        gather_cc(0, 0, I)
+        result(0, 0, I, nc.gpsimd)
+        difference(1, nc.gpsimd)
+        weigh(0, 0, I, nc.gpsimd)
+        rival(3)
+        place_v(3)
+        gather_cc(1, 0, I)
+        result(1, 0, I, nc.gpsimd)
+        difference(2, nc.gpsimd)
+        weigh(1, 0, I, nc.gpsimd)
+        gather_cc(2, 0, I)
+        difference(3, nc.vector)
+        for lo in (0, HALF):
+            gather_cc(3, lo, lo + HALF)
+        result(2, 0, I, nc.vector)
+        weigh(2, 0, I, nc.vector)
+        for lo in (0, HALF):
+            result(3, lo, lo + HALF, nc.vector)
+            weigh(3, lo, lo + HALF, nc.vector)
+
+        for n in range(2):
+            lo = n * HALF
+            woven = tile([P, HALF * PACK], BF16, "woven%d" % n)
+            nc.vector.tensor_copy(out=woven[:].rearrange("p (c i r) -> p c r i", i=4, r=PACK),
+                                  in_=gw[:, :, lo:lo + HALF].rearrange("p r (c i) -> p c r i", i=4))
+            codes = tile([P, HALF], U32, "gw_codes%d" % n)
+            plane = tile([P, HALF], U8, "gw_plane%d" % n)
+            nc.vector.quantize_mx(out=codes[:].bitcast(FP8X4), scales=plane[:], in_=woven[:])
+            for e in range(2):
+                chans = slice(e * P, (e + 1) * P)
+                bank = ps.tile([P, HALF], F32, name="bank_a" if e == 0 else "bank_b")
+                nc.tensor.matmul_mx(out=bank[:], lhsT=mix[:, chans].bitcast(FP8X4), lhsT_scale=mix_plane[:, chans],
+                                    rhs=codes[:].bitcast(FP8X4), rhs_scale=plane[:], start=True, stop=True)
+                y = tile([P, HALF], F32, "y%d_%d" % (n, e))
+                if n == 1 and e == 1:
+                    nc.vector.tensor_copy(y[:], bank[:])
+                else:
+                    nc.scalar.activation(y[:], bank[:], COPY)
+                nc.sync.dma_start(out=out[chans, lo:lo + HALF], in_=y[:])

@@ -29,7 +29,7 @@ def tile_attend_auction_twoq_mixed_kernel(tc, query, query2, keys_words, keys_sc
     nc = tc.nc
     with ExitStack() as ctx:
         sb = ctx.enter_context(tc.tile_pool(name="sb", bufs=1))
-        ps = ctx.enter_context(tc.psum_pool(name="ps", bufs=4))
+        ps = ctx.enter_context(tc.psum_pool(name="ps", bufs=1))
 
         def tile(shape, dtype, name, tag=None):
             return sb.tile(shape, dtype, name=name, tag=tag or name, align_bytes=64)
@@ -50,40 +50,45 @@ def tile_attend_auction_twoq_mixed_kernel(tc, query, query2, keys_words, keys_sc
                 engine.dma_start(out=plane[f:P:32, :].bitcast(I32), in_=rows[f])
 
         def load_query(src, name):
-            rows = src.rearrange("(p j) q -> p j q", j=PACK)
-            halves = []
-            for u in range(2):
-                raw = tile([P, 2, Q], F32, name + "_raw%d" % u)
-                nc.sync.dma_start(out=raw[:], in_=rows[:, 2 * u:2 * u + 2, :])
-                halves.append(raw)
-            return halves
+            raw = tile([P, PACK, Q], F32, name + "_raw")
+            nc.sync.dma_start(out=raw[:], in_=src.rearrange("(p j) q -> p j q", j=PACK))
+            return raw
 
-        def cast_query(halves, name):
+        def quantize_query(raw, name):
             grouped = tile([P, Q * PACK], BF16, name + "_bf")
-            dst = grouped[:].rearrange("p (r m j) -> p m r j", r=PACK, j=PACK)
-            for u in range(2):
-                nc.vector.tensor_copy(out=dst[:, :, :, 2 * u:2 * u + 2],
-                                      in_=halves[u][:].rearrange("p j (m r) -> p m r j", r=PACK))
             codes = tile([P, Q], U32, name + "_codes")
             plane = tile([P, Q], U8, name + "_plane")
-            for lo, hi in ((0, P), (P, 2 * P), (2 * P, 4 * P)):
-                nc.vector.quantize_mx(out=codes[:, lo:hi].bitcast(FP8X4), scales=plane[:, lo:hi],
-                                      in_=grouped[:, PACK * lo:PACK * hi])
+            dst = grouped[:].rearrange("p (r m j) -> p m r j", r=PACK, j=PACK)
+            src = raw[:].rearrange("p j (m r) -> p m r j", r=PACK)
+
+            def cast(lo, hi):
+                nc.vector.tensor_copy(out=dst[:, :, lo:hi, :], in_=src[:, :, lo:hi, :])
+
+            def quantize(lo, hi):
+                nc.vector.quantize_mx(out=codes[:, lo * P:hi * P].bitcast(FP8X4), scales=plane[:, lo * P:hi * P],
+                                      in_=grouped[:, PACK * P * lo:PACK * P * hi])
+
+            cast(0, 1)
+            cast(1, 2)
+            quantize(0, 1)
+            cast(2, 4)
+            quantize(1, 2)
+            quantize(2, 4)
             return codes, plane
 
-        notes_plane = zeroed_plane(T, "notes_plane")
         keys_plane = zeroed_plane(T, "keys_plane")
-        lst2 = load_list(offs2, "lst2")
-        load_plane(nc.scalar, notes_plane, notes_scales)
-        q2_raw = load_query(query2, "q2")
-        notes = tile([P, T], I32, "notes")
-        nc.sync.dma_start(out=notes[:], in_=notes_words[0].rearrange("p n t -> p (n t)").bitcast(I32))
-        load_plane(nc.scalar, keys_plane, keys_scales)
+        notes_plane = zeroed_plane(T, "notes_plane")
         q1_raw = load_query(query, "q1")
+        load_plane(nc.sync, keys_plane, keys_scales)
         keys = tile([P, 2 * T], U8, "keys")
         nc.sync.dma_start(out=keys[:].bitcast(I32), in_=keys_words[0].bitcast(I32))
         lst1 = load_list(offs, "lst1")
+        q2_raw = load_query(query2, "q2")
+        lst2 = load_list(offs2, "lst2")
         lst3 = load_list(offs3, "lst3")
+        load_plane(nc.sync, notes_plane, notes_scales)
+        notes = tile([P, T], I32, "notes")
+        nc.sync.dma_start(out=notes[:], in_=notes_words[0].rearrange("p n t -> p (n t)").bitcast(I32))
         lst4 = load_list(offs4, "lst4")
         lst5 = load_list(offs5, "lst5")
         lst6 = load_list(offs6, "lst6")
@@ -92,129 +97,161 @@ def tile_attend_auction_twoq_mixed_kernel(tc, query, query2, keys_words, keys_sc
         mix = tile([P, E], I32, "mix")
         nc.sync.dma_start(out=mix[:], in_=mix_words[0].rearrange("p n t -> p (n t)").bitcast(I32))
 
-        q2_codes, q2_plane = cast_query(q2_raw, "q2")
-        q1_codes, q1_plane = cast_query(q1_raw, "q1")
+        q1_codes, q1_plane = quantize_query(q1_raw, "q1")
+        q2_codes, q2_plane = quantize_query(q2_raw, "q2")
 
-        a = [tile([P, T], F32, "a%d" % r) for r in range(PACK)]
-        b = [tile([P, T], F32, "b%d" % r) for r in range(2)]
-        b += [tile([P, T], F32, "b%d" % r, tag="a%d" % (r - 2)) for r in range(2, PACK)]
-        f1 = [tile([P, Z], F32, "f1_0"), tile([P, Z], F32, "f1_1"), tile([P, Z], F32, "f1_2", tag="b1")]
-        f2 = [tile([P, Z], F32, "f2_0", tag="q1_bf"), tile([P, Z], F32, "f2_1", tag="a2")]
-        cc = [tile([P, Z], F32, "cc%d" % r) for r in range(PACK)]
-        ga = [tile([P, I], F32, "ga%d" % r) for r in range(PACK)]
-        gb = [tile([P, I], F32, "gb%d" % r) for r in range(PACK)]
-        w = [tile([P, I], F32, "w%d" % r) for r in range(PACK)]
-        gf = [tile([P, I], F32, "gf%d" % r) for r in range(PACK)]
-        v = [tile([P, I], F32, "v%d" % r) for r in range(PACK)]
-        gc = [tile([P, I], F32, "gc%d" % r) for r in range(PACK)]
-        g = [tile([P, I], F32, "g%d" % r) for r in range(PACK)]
+        banks = [ps.tile([P, BANK], F32, name="bank%d" % n) for n in range(8)]
+        takes_over = {"ga1_0": "b0", "ga1_256": "b0", "a2": "ga0_0", "b2": "a1", "a3": "gb1_256", "b3": "a2",
+                      "f1_2": "gb0_256", "f2_0": "q2_bf", "f2_1": "gf0_256", "v1": "gb2_256", "cc0": "gf1_0",
+                      "v2": "gb3_256", "g0": "gf2_0", "cc1": "gc0_0", "v3": "f1_1", "g1": "gf3_256", "cc2": "gc1_0",
+                      "gc3_256": "gc1_0"}
+        takes_over["ga1_256"] = "ga0_0"
+        takes_over["a2"] = takes_over["b3"] = "gb1_0"
+        made = {}
+
+        def held(name, width):
+            if name not in made:
+                made[name] = tile([P, width], F32, name, tag=takes_over.get(name))
+            return made[name]
+
+        def window(kind, r):
+            return held(kind + str(r), Z)
+
+        def dense(kind, r, lo, hi):
+            return held(kind + str(r), I)[:, lo:hi]
+
+        def gathered(kind, r, lo, hi):
+            return held("%s%d_%d" % (kind, r, lo), hi - lo)[:]
+
         gw = tile([P, PACK, I], BF16, "gw")
 
-        def scores_b(r):
-            rows = slice(r * P, (r + 1) * P)
-            for h in range(2):
-                cols = slice(h * BANK, (h + 1) * BANK)
-                bank = ps.tile([P, BANK], F32, name="bank_b")
-                nc.tensor.matmul_mx(out=bank[:], lhsT=q2_codes[:, rows].bitcast(FP8X4), lhsT_scale=q2_plane[:, rows],
-                                    rhs=notes[:, cols].bitcast(FP8X4), rhs_scale=notes_plane[:, cols],
-                                    start=True, stop=True)
-                nc.scalar.activation(b[r][:, cols], bank[:], COPY)
+        HALVES = ((0, HALF), (HALF, I))
+
+        def empty_bank(dst, bank, on_vector):
+            if on_vector:
+                nc.vector.tensor_copy(dst, bank)
+            else:
+                nc.scalar.activation(dst, bank, COPY)
 
         def scores_a(r):
             rows = slice(r * P, (r + 1) * P)
             for h in range(2):
                 cols = slice(h * BANK, (h + 1) * BANK)
-                bank = ps.tile([P, BANK], F32, name="bank_a")
+                bank = banks[(2 * r + h) % 8]
                 nc.tensor.matmul_mx(out=bank[:], lhsT=q1_codes[:, rows].bitcast(FP8X4), lhsT_scale=q1_plane[:, rows],
                                     rhs=keys[:, 2 * h * BANK:2 * (h + 1) * BANK].bitcast(FP4X4),
                                     rhs_scale=keys_plane[:, cols], start=True, stop=True)
-                if r == 0 and h == 0:
-                    nc.vector.tensor_copy(a[r][:, cols], bank[:])
-                else:
-                    nc.scalar.activation(a[r][:, cols], bank[:], COPY)
+                empty_bank(window("a", r)[:, cols], bank[:], (r, h) == (1, 1))
 
-        def gather_b(r):
-            nc.scalar.activation(gb[r][:], b[r][:].indirect(lst2[:]), COPY)
+        def scores_b(r):
+            rows = slice(r * P, (r + 1) * P)
+            for h in range(2):
+                cols = slice(h * BANK, (h + 1) * BANK)
+                bank = banks[(2 * r + h + 4) % 8]
+                nc.tensor.matmul_mx(out=bank[:], lhsT=q2_codes[:, rows].bitcast(FP8X4), lhsT_scale=q2_plane[:, rows],
+                                    rhs=notes[:, cols].bitcast(FP8X4), rhs_scale=notes_plane[:, cols],
+                                    start=True, stop=True)
+                empty_bank(window("b", r)[:, cols], bank[:], (r, h) == (0, 0))
 
-        def bids(r):
-            nc.scalar.activation(ga[r][:], a[r][:].indirect(lst1[:]), COPY)
-            nc.gpsimd.tensor_tensor(w[r][:], ga[r][:], gb[r][:], ADD)
+        def listed(win, lst, lo, hi):
+            return win[:].indirect(lst[:, lo // 16:hi // 16])
 
-        def place_w(r):
-            nc.vector.tensor_copy(f1[r % 3][:].indirect(lst3[:]), w[r][:])
+        def f1(r):
+            return window("f1_", r % 3)
 
-        def rival(r):
-            nc.scalar.activation(gf[r][:], f1[r % 3][:].indirect(lst4[:]), COPY)
-            nc.gpsimd.tensor_tensor(v[r][:], gf[r][:], w[r][:], SUB)
+        def f2(r):
+            return window("f2_", r % 2)
+
+        def gather(kind, r, win, lst, lo, hi):
+            nc.scalar.activation(gathered(kind, r, lo, hi), listed(win, lst, lo, hi), COPY)
+
+        def bids(r, lo, hi):
+            gather("ga", r, window("a", r), lst1, lo, hi)
+            gather("gb", r, window("b", r), lst2, lo, hi)
+            nc.gpsimd.tensor_tensor(dense("w", r, lo, hi), gathered("ga", r, lo, hi), gathered("gb", r, lo, hi), ADD)
+
+        def place_w(r, lo, hi):
+            nc.vector.tensor_copy(listed(f1(r), lst3, lo, hi), dense("w", r, lo, hi))
+
+        def rival(r, lo, hi):
+            gather("gf", r, f1(r), lst4, lo, hi)
+            nc.gpsimd.tensor_tensor(dense("v", r, lo, hi), gathered("gf", r, lo, hi), dense("w", r, lo, hi), SUB)
 
         def place_v(r):
-            nc.vector.tensor_copy(f2[r % 2][:].indirect(lst5[:]), v[r][:])
+            nc.vector.tensor_copy(listed(f2(r), lst5, 0, I), dense("v", r, 0, I))
 
         def difference(r, engine):
-            engine.tensor_tensor(cc[r][:], f1[r % 3][:], f2[r % 2][:], SUB)
+            engine.tensor_tensor(window("cc", r)[:], f1(r)[:], f2(r)[:], SUB)
 
         def gather_cc(r, lo, hi):
-            nc.scalar.activation(gc[r][:, lo:hi], cc[r][:].indirect(lst6[:, lo // 16:hi // 16]), COPY)
+            gather("gc", r, window("cc", r), lst6, lo, hi)
 
         def result(r, lo, hi, engine):
-            engine.tensor_tensor(g[r][:, lo:hi], gc[r][:, lo:hi], w[r][:, lo:hi], ADD)
+            engine.tensor_tensor(dense("g", r, lo, hi), gathered("gc", r, lo, hi), dense("w", r, lo, hi), ADD)
 
-        def weigh(r, lo, hi, engine):
-            engine.tensor_scalar(gw[:, r, lo:hi], g[r][:, lo:hi], factor[:, r:r + 1], 0.0, MUL, ADD)
+        def weigh_scalar(r):
+            nc.scalar.activation(gw[:, r, :], dense("g", r, 0, I), COPY, scale=factor[:, r:r + 1])
 
-        nc.vector.memset(f1[0][:], 0.0)
-        nc.vector.memset(f1[1][:], 0.0)
+        nc.vector.memset(f1(0)[:], 0.0)
+        nc.vector.memset(f1(1)[:], 0.0)
         mix_plane = zeroed_plane(E, "mix_plane")
         load_plane(nc.sync, mix_plane, mix_scales)
-        scores_b(0)
-        gather_b(0)
-        scores_b(1)
         scores_a(0)
-        nc.vector.tensor_tensor(w[0][:], a[0][:].indirect(lst1[:]), gb[0][:], ADD)
-        place_w(0)
-        nc.gpsimd.memset(f2[0][:], 0.0)
-        gather_b(1)
-        nc.gpsimd.memset(f1[2][:], 0.0)
+        gather("ga", 0, window("a", 0), lst1, 0, I)
         scores_a(1)
-        bids(1)
-        place_w(1)
-        scores_b(2)
-        rival(0)
-        place_v(0)
+        scores_b(0)
+        ga0 = gathered("ga", 0, 0, I)
+        nc.vector.tensor_tensor(dense("w", 0, 0, HALF), listed(window("b", 0), lst2, 0, HALF), ga0[:, :HALF], ADD)
+        gather("gb", 0, window("b", 0), lst2, HALF, I)
+        nc.gpsimd.tensor_tensor(dense("w", 0, HALF, I), ga0[:, HALF:], gathered("gb", 0, HALF, I), ADD)
+        for lo, hi in HALVES:
+            place_w(0, lo, hi)
+        nc.gpsimd.memset(f2(0)[:], 0.0)
+        nc.gpsimd.memset(f1(2)[:], 0.0)
+        scores_b(1)
+        for lo, hi in HALVES:
+            bids(1, lo, hi)
+        for lo, hi in HALVES:
+            place_w(1, lo, hi)
         scores_a(2)
-        gather_b(2)
-        bids(2)
-        nc.gpsimd.memset(f2[1][:], 0.0)
-        place_w(2)
-        rival(1)
+        for lo, hi in HALVES:
+            rival(0, lo, hi)
+        place_v(0)
+        nc.gpsimd.memset(f2(1)[:], 0.0)
+        scores_b(2)
+        for lo, hi in HALVES:
+            bids(2, lo, hi)
+        place_w(2, 0, I)
+        rival(1, 0, I)
         place_v(1)
         difference(0, nc.gpsimd)
-        scores_b(3)
         scores_a(3)
-        gather_b(3)
-        bids(3)
-        place_w(3)
-        rival(2)
+        scores_b(3)
+        for lo, hi in HALVES:
+            bids(3, lo, hi)
+        place_w(3, 0, I)
+        rival(2, 0, I)
         place_v(2)
         gather_cc(0, 0, I)
         result(0, 0, I, nc.gpsimd)
         difference(1, nc.gpsimd)
-        weigh(0, 0, I, nc.gpsimd)
-        rival(3)
+        for lo, hi in HALVES:
+            rival(3, lo, hi)
         place_v(3)
+        weigh_scalar(0)
         gather_cc(1, 0, I)
         result(1, 0, I, nc.gpsimd)
         difference(2, nc.gpsimd)
-        weigh(1, 0, I, nc.gpsimd)
+        weigh_scalar(1)
         gather_cc(2, 0, I)
         difference(3, nc.vector)
-        for lo in (0, HALF):
-            gather_cc(3, lo, lo + HALF)
+        nc.vector.tensor_tensor(dense("g", 3, 0, HALF), listed(window("cc", 3), lst6, 0, HALF), dense("w", 3, 0, HALF), ADD)
+        gather_cc(3, HALF, I)
         result(2, 0, I, nc.vector)
-        weigh(2, 0, I, nc.vector)
-        for lo in (0, HALF):
-            result(3, lo, lo + HALF, nc.vector)
-            weigh(3, lo, lo + HALF, nc.vector)
+        weigh_scalar(2)
+        result(3, HALF, I, nc.vector)
+        for lo, hi in HALVES:
+            nc.vector.tensor_scalar(gw[:, 3, lo:hi], dense("g", 3, lo, hi), factor[:, 3:4], 0.0, MUL, ADD)
 
         for n in range(2):
             lo = n * HALF
@@ -226,12 +263,9 @@ def tile_attend_auction_twoq_mixed_kernel(tc, query, query2, keys_words, keys_sc
             nc.vector.quantize_mx(out=codes[:].bitcast(FP8X4), scales=plane[:], in_=woven[:])
             for e in range(2):
                 chans = slice(e * P, (e + 1) * P)
-                bank = ps.tile([P, HALF], F32, name="bank_a" if e == 0 else "bank_b")
-                nc.tensor.matmul_mx(out=bank[:], lhsT=mix[:, chans].bitcast(FP8X4), lhsT_scale=mix_plane[:, chans],
+                bank = banks[2 * n + e][:, :HALF]
+                nc.tensor.matmul_mx(out=bank, lhsT=mix[:, chans].bitcast(FP8X4), lhsT_scale=mix_plane[:, chans],
                                     rhs=codes[:].bitcast(FP8X4), rhs_scale=plane[:], start=True, stop=True)
                 y = tile([P, HALF], F32, "y%d_%d" % (n, e))
-                if n == 1 and e == 1:
-                    nc.vector.tensor_copy(y[:], bank[:])
-                else:
-                    nc.scalar.activation(y[:], bank[:], COPY)
+                empty_bank(y[:], bank, (n, e) == (1, 1))
                 nc.sync.dma_start(out=out[chans, lo:lo + HALF], in_=y[:])

@@ -101,12 +101,10 @@ def tile_attend_auction_twoq_mixed_kernel(tc, query, query2, keys_words, keys_sc
         q2_codes, q2_plane = quantize_query(q2_raw, "q2")
 
         banks = [ps.tile([P, BANK], F32, name="bank%d" % n) for n in range(8)]
-        takes_over = {"ga1_0": "b0", "ga1_256": "b0", "a2": "ga0_0", "b2": "a1", "a3": "gb1_256", "b3": "a2",
+        takes_over = {"ga1_0": "b0", "ga1_256": "ga0_0", "a2": "gb1_0", "b2": "a1", "a3": "gb1_256", "b3": "gb1_0",
                       "f1_2": "gb0_256", "f2_0": "q2_bf", "f2_1": "gf0_256", "v1": "gb2_256", "cc0": "gf1_0",
-                      "v2": "gb3_256", "g0": "gf2_0", "cc1": "gc0_0", "v3": "f1_1", "g1": "gf3_256", "cc2": "gc1_0",
-                      "gc3_256": "gc1_0"}
-        takes_over["ga1_256"] = "ga0_0"
-        takes_over["a2"] = takes_over["b3"] = "gb1_0"
+                      "v2": "gb3_256", "g0": "gf2_0", "cc1": "gc0_0", "v3": "f1_1", "cc2": "gf3_256",
+                      "gc3_256": "gf3_256", "g1": "gb0_256", "g2": "f1_1"}
         made = {}
 
         def held(name, width):
@@ -192,6 +190,9 @@ def tile_attend_auction_twoq_mixed_kernel(tc, query, query2, keys_words, keys_sc
         def weigh_scalar(r):
             nc.scalar.activation(gw[:, r, :], dense("g", r, 0, I), COPY, scale=factor[:, r:r + 1])
 
+        def weigh_vector(r, lo, hi):
+            nc.vector.tensor_scalar(gw[:, r, lo:hi], dense("g", r, lo, hi), factor[:, r:r + 1], 0.0, MUL, ADD)
+
         nc.vector.memset(f1(0)[:], 0.0)
         nc.vector.memset(f1(1)[:], 0.0)
         mix_plane = zeroed_plane(E, "mix_plane")
@@ -240,18 +241,18 @@ def tile_attend_auction_twoq_mixed_kernel(tc, query, query2, keys_words, keys_sc
         place_v(3)
         weigh_scalar(0)
         gather_cc(1, 0, I)
-        result(1, 0, I, nc.gpsimd)
         difference(2, nc.gpsimd)
-        weigh_scalar(1)
+        result(1, 0, I, nc.gpsimd)
         gather_cc(2, 0, I)
+        weigh_scalar(1)
         difference(3, nc.vector)
-        nc.vector.tensor_tensor(dense("g", 3, 0, HALF), listed(window("cc", 3), lst6, 0, HALF), dense("w", 3, 0, HALF), ADD)
         gather_cc(3, HALF, I)
         result(2, 0, I, nc.vector)
+        nc.vector.tensor_tensor(dense("g", 3, 0, HALF), listed(window("cc", 3), lst6, 0, HALF), dense("w", 3, 0, HALF), ADD)
         weigh_scalar(2)
         result(3, HALF, I, nc.vector)
         for lo, hi in HALVES:
-            nc.vector.tensor_scalar(gw[:, 3, lo:hi], dense("g", 3, lo, hi), factor[:, 3:4], 0.0, MUL, ADD)
+            weigh_vector(3, lo, hi)
 
         for n in range(2):
             lo = n * HALF

@@ -149,7 +149,7 @@ def tile_attend_auction_twoq_mixed_kernel(tc, query, query2, keys_words, keys_sc
                 nc.tensor.matmul_mx(out=bank[:], lhsT=q2_codes[:, rows].bitcast(FP8X4), lhsT_scale=q2_plane[:, rows],
                                     rhs=notes[:, cols].bitcast(FP8X4), rhs_scale=notes_plane[:, cols],
                                     start=True, stop=True)
-                empty_bank(window("b", r)[:, cols], bank[:], (r, h) == (0, 0))
+                empty_bank(window("b", r)[:, cols], bank[:], (r, h) in ((0, 0), (2, 0)))
 
         def listed(win, lst, lo, hi):
             return win[:].indirect(lst[:, lo // 16:hi // 16])
@@ -175,8 +175,8 @@ def tile_attend_auction_twoq_mixed_kernel(tc, query, query2, keys_words, keys_sc
             gather("gf", r, f1(r), lst4, lo, hi)
             nc.gpsimd.tensor_tensor(dense("v", r, lo, hi), gathered("gf", r, lo, hi), dense("w", r, lo, hi), SUB)
 
-        def place_v(r):
-            nc.vector.tensor_copy(listed(f2(r), lst5, 0, I), dense("v", r, 0, I))
+        def place_v(r, lo=0, hi=I):
+            nc.vector.tensor_copy(listed(f2(r), lst5, lo, hi), dense("v", r, lo, hi))
 
         def difference(r, engine):
             engine.tensor_tensor(window("cc", r)[:], f1(r)[:], f2(r)[:], SUB)
@@ -238,7 +238,8 @@ def tile_attend_auction_twoq_mixed_kernel(tc, query, query2, keys_words, keys_sc
         difference(1, nc.gpsimd)
         for lo, hi in HALVES:
             rival(3, lo, hi)
-        place_v(3)
+        for lo, hi in HALVES:
+            place_v(3, lo, hi)
         weigh_scalar(0)
         gather_cc(1, 0, I)
         difference(2, nc.gpsimd)

from contextlib import ExitStack

import concourse.mybir as mybir

D, T, Z, I, Q, E = 512, 1024, 1024, 512, 512, 256
FLOPS = 2 * D * Q * T * 2 + 2 * Q * E * I

F32 = mybir.dt.float32
BF16 = mybir.dt.bfloat16
I32 = mybir.dt.int32
U32 = mybir.dt.uint32
U16 = mybir.dt.uint16
U8 = mybir.dt.uint8
FP8X4 = mybir.dt.float8_e4m3fn_x4
FP4X4 = mybir.dt.float4_e2m1fn_x4
ADD = mybir.AluOpType.add
SUB = mybir.AluOpType.subtract
MUL = mybir.AluOpType.mult
COPY = mybir.ActivationFunctionType.Copy

P = 128
PACK = 4
BANK = 512
HALF = I // 2


def tile_attend_auction_twoq_mixed_kernel(tc, query, query2, keys_words, keys_scales, notes_words, notes_scales,
                                           rowf, mix_words, mix_scales, offs, offs2, offs3, offs4, offs5, offs6, out):
    nc = tc.nc
    with ExitStack() as ctx:
        sb = ctx.enter_context(tc.tile_pool(name="sb", bufs=1))
        ps = ctx.enter_context(tc.psum_pool(name="ps", bufs=1))

        def tile(shape, dtype, name, tag=None):
            return sb.tile(shape, dtype, name=name, tag=tag or name, align_bytes=64)

        def load_list(src, name):
            lst = sb.tile([P, I // 16], U16, name=name)
            nc.sync.dma_start(lst[:], src)
            return lst

        def zeroed_plane(width, name):
            plane = tile([P, width], U8, name)
            nc.vector.memset(plane[:].bitcast(U32), 0)
            return plane

        def load_plane(engine, plane, scales):
            rows = scales[0].bitcast(I32).rearrange("(b f) c -> f b c", f=4)
            for f in range(4):
                engine.dma_start(out=plane[f:P:32, :].bitcast(I32), in_=rows[f])

        def load_query(src, name):
            raw = tile([P, PACK, Q], F32, name + "_raw")
            nc.sync.dma_start(out=raw[:], in_=src.rearrange("(p j) q -> p j q", j=PACK))
            return raw

        def quantize_query(raw, name):
            grouped = tile([P, Q * PACK], BF16, name + "_bf")
            codes = tile([P, Q], U32, name + "_codes")
            plane = tile([P, Q], U8, name + "_plane")
            dst = grouped[:].rearrange("p (r m j) -> p m r j", r=PACK, j=PACK)
            src = raw[:].rearrange("p j (m r) -> p m r j", r=PACK)

            def cast(lo, hi):
                nc.vector.tensor_copy(out=dst[:, :, lo:hi, :], in_=src[:, :, lo:hi, :])

            def quantize(lo, hi):
                nc.vector.quantize_mx(out=codes[:, lo * P:hi * P].bitcast(FP8X4), scales=plane[:, lo * P:hi * P],
                                      in_=grouped[:, PACK * P * lo:PACK * P * hi])

            cast(0, 1)
            cast(1, 2)
            quantize(0, 1)
            cast(2, 4)
            quantize(1, 2)
            quantize(2, 4)
            return codes, plane

        keys_plane = zeroed_plane(T, "keys_plane")
        notes_plane = zeroed_plane(T, "notes_plane")
        q1_raw = load_query(query, "q1")
        load_plane(nc.sync, keys_plane, keys_scales)
        keys = tile([P, 2 * T], U8, "keys")
        nc.sync.dma_start(out=keys[:].bitcast(I32), in_=keys_words[0].bitcast(I32))
        lst1 = load_list(offs, "lst1")
        q2_raw = load_query(query2, "q2")
        lst2 = load_list(offs2, "lst2")
        lst3 = load_list(offs3, "lst3")
        load_plane(nc.sync, notes_plane, notes_scales)
        notes = tile([P, T], I32, "notes")
        nc.sync.dma_start(out=notes[:], in_=notes_words[0].rearrange("p n t -> p (n t)").bitcast(I32))
        lst4 = load_list(offs4, "lst4")
        lst5 = load_list(offs5, "lst5")
        lst6 = load_list(offs6, "lst6")
        factor = tile([P, PACK], F32, "factor")
        nc.sync.dma_start(out=factor[:], in_=rowf.rearrange("(p r) o -> p (r o)", r=PACK))
        mix = tile([P, E], I32, "mix")
        nc.sync.dma_start(out=mix[:], in_=mix_words[0].rearrange("p n t -> p (n t)").bitcast(I32))

        q1_codes, q1_plane = quantize_query(q1_raw, "q1")
        q2_codes, q2_plane = quantize_query(q2_raw, "q2")

        banks = [ps.tile([P, BANK], F32, name="bank%d" % n) for n in range(8)]
        takes_over = {"ga1_0": "b0", "ga1_256": "ga0_0", "a2": "gb1_0", "b2": "a1", "a3": "gb1_256", "b3": "gb1_0",
                      "f1_2": "gb0_256", "f2_0": "q2_bf", "f2_1": "gf0_256", "v1": "gb2_256", "cc0": "gf1_0",
                      "v2": "gb3_256", "g0": "gf2_0", "cc1": "gc0_0", "v3": "f1_1", "cc2": "gf3_256",
                      "gc3_256": "gf3_256", "g1": "gb0_256", "g2": "f1_1"}
        made = {}

        def held(name, width):
            if name not in made:
                made[name] = tile([P, width], F32, name, tag=takes_over.get(name))
            return made[name]

        def window(kind, r):
            return held(kind + str(r), Z)

        def dense(kind, r, lo, hi):
            return held(kind + str(r), I)[:, lo:hi]

        def gathered(kind, r, lo, hi):
            return held("%s%d_%d" % (kind, r, lo), hi - lo)[:]

        gw = tile([P, PACK, I], BF16, "gw")

        HALVES = ((0, HALF), (HALF, I))

        def empty_bank(dst, bank, on_vector):
            if on_vector:
                nc.vector.tensor_copy(dst, bank)
            else:
                nc.scalar.activation(dst, bank, COPY)

        def scores_a(r):
            rows = slice(r * P, (r + 1) * P)
            for h in range(2):
                cols = slice(h * BANK, (h + 1) * BANK)
                bank = banks[(2 * r + h) % 8]
                nc.tensor.matmul_mx(out=bank[:], lhsT=q1_codes[:, rows].bitcast(FP8X4), lhsT_scale=q1_plane[:, rows],
                                    rhs=keys[:, 2 * h * BANK:2 * (h + 1) * BANK].bitcast(FP4X4),
                                    rhs_scale=keys_plane[:, cols], start=True, stop=True)
                empty_bank(window("a", r)[:, cols], bank[:], (r, h) == (1, 1))

        def scores_b(r):
            rows = slice(r * P, (r + 1) * P)
            for h in range(2):
                cols = slice(h * BANK, (h + 1) * BANK)
                bank = banks[(2 * r + h + 4) % 8]
                nc.tensor.matmul_mx(out=bank[:], lhsT=q2_codes[:, rows].bitcast(FP8X4), lhsT_scale=q2_plane[:, rows],
                                    rhs=notes[:, cols].bitcast(FP8X4), rhs_scale=notes_plane[:, cols],
                                    start=True, stop=True)
                empty_bank(window("b", r)[:, cols], bank[:], (r, h) in ((0, 0), (2, 0)))

        def listed(win, lst, lo, hi):
            return win[:].indirect(lst[:, lo // 16:hi // 16])

        def f1(r):
            return window("f1_", r % 3)

        def f2(r):
            return window("f2_", r % 2)

        def gather(kind, r, win, lst, lo, hi):
            nc.scalar.activation(gathered(kind, r, lo, hi), listed(win, lst, lo, hi), COPY)

        def bids(r, lo, hi):
            gather("ga", r, window("a", r), lst1, lo, hi)
            gather("gb", r, window("b", r), lst2, lo, hi)
            nc.gpsimd.tensor_tensor(dense("w", r, lo, hi), gathered("ga", r, lo, hi), gathered("gb", r, lo, hi), ADD)

        def place_w(r, lo, hi):
            nc.vector.tensor_copy(listed(f1(r), lst3, lo, hi), dense("w", r, lo, hi))

        def rival(r, lo, hi):
            gather("gf", r, f1(r), lst4, lo, hi)
            nc.gpsimd.tensor_tensor(dense("v", r, lo, hi), gathered("gf", r, lo, hi), dense("w", r, lo, hi), SUB)

        def place_v(r, lo=0, hi=I):
            nc.vector.tensor_copy(listed(f2(r), lst5, lo, hi), dense("v", r, lo, hi))

        def difference(r, engine):
            engine.tensor_tensor(window("cc", r)[:], f1(r)[:], f2(r)[:], SUB)

        def gather_cc(r, lo, hi):
            gather("gc", r, window("cc", r), lst6, lo, hi)

        def result(r, lo, hi, engine):
            engine.tensor_tensor(dense("g", r, lo, hi), gathered("gc", r, lo, hi), dense("w", r, lo, hi), ADD)

        def weigh_scalar(r):
            nc.scalar.activation(gw[:, r, :], dense("g", r, 0, I), COPY, scale=factor[:, r:r + 1])

        def weigh_vector(r, lo, hi):
            nc.vector.tensor_scalar(gw[:, r, lo:hi], dense("g", r, lo, hi), factor[:, r:r + 1], 0.0, MUL, ADD)

        nc.vector.memset(f1(0)[:], 0.0)
        nc.vector.memset(f1(1)[:], 0.0)
        mix_plane = zeroed_plane(E, "mix_plane")
        load_plane(nc.sync, mix_plane, mix_scales)
        scores_a(0)
        gather("ga", 0, window("a", 0), lst1, 0, I)
        scores_a(1)
        scores_b(0)
        ga0 = gathered("ga", 0, 0, I)
        nc.vector.tensor_tensor(dense("w", 0, 0, HALF), listed(window("b", 0), lst2, 0, HALF), ga0[:, :HALF], ADD)
        gather("gb", 0, window("b", 0), lst2, HALF, I)
        nc.gpsimd.tensor_tensor(dense("w", 0, HALF, I), ga0[:, HALF:], gathered("gb", 0, HALF, I), ADD)
        for lo, hi in HALVES:
            place_w(0, lo, hi)
        nc.gpsimd.memset(f2(0)[:], 0.0)
        nc.gpsimd.memset(f1(2)[:], 0.0)
        scores_b(1)
        for lo, hi in HALVES:
            bids(1, lo, hi)
        for lo, hi in HALVES:
            place_w(1, lo, hi)
        scores_a(2)
        for lo, hi in HALVES:
            rival(0, lo, hi)
        place_v(0)
        nc.gpsimd.memset(f2(1)[:], 0.0)
        scores_b(2)
        for lo, hi in HALVES:
            bids(2, lo, hi)
        place_w(2, 0, I)
        rival(1, 0, I)
        place_v(1)
        difference(0, nc.gpsimd)
        scores_a(3)
        scores_b(3)
        for lo, hi in HALVES:
            bids(3, lo, hi)
        place_w(3, 0, I)
        rival(2, 0, I)
        place_v(2)
        gather_cc(0, 0, I)
        result(0, 0, I, nc.gpsimd)
        difference(1, nc.gpsimd)
        for lo, hi in HALVES:
            rival(3, lo, hi)
        for lo, hi in HALVES:
            place_v(3, lo, hi)
        weigh_scalar(0)
        gather_cc(1, 0, I)
        difference(2, nc.gpsimd)
        result(1, 0, I, nc.gpsimd)
        gather_cc(2, 0, I)
        weigh_scalar(1)
        difference(3, nc.vector)
        gather_cc(3, HALF, I)
        result(2, 0, I, nc.vector)
        nc.vector.tensor_tensor(dense("g", 3, 0, HALF), listed(window("cc", 3), lst6, 0, HALF), dense("w", 3, 0, HALF), ADD)
        weigh_scalar(2)
        result(3, HALF, I, nc.vector)
        for lo, hi in HALVES:
            weigh_vector(3, lo, hi)

        for n in range(2):
            lo = n * HALF
            woven = tile([P, HALF * PACK], BF16, "woven%d" % n)
            nc.vector.tensor_copy(out=woven[:].rearrange("p (c i r) -> p c r i", i=4, r=PACK),
                                  in_=gw[:, :, lo:lo + HALF].rearrange("p r (c i) -> p c r i", i=4))
            codes = tile([P, HALF], U32, "gw_codes%d" % n)
            plane = tile([P, HALF], U8, "gw_plane%d" % n)
            nc.vector.quantize_mx(out=codes[:].bitcast(FP8X4), scales=plane[:], in_=woven[:])
            for e in range(2):
                chans = slice(e * P, (e + 1) * P)
                bank = banks[2 * n + e][:, :HALF]
                nc.tensor.matmul_mx(out=bank, lhsT=mix[:, chans].bitcast(FP8X4), lhsT_scale=mix_plane[:, chans],
                                    rhs=codes[:].bitcast(FP8X4), rhs_scale=plane[:], start=True, stop=True)
                y = tile([P, HALF], F32, "y%d_%d" % (n, e))
                empty_bank(y[:], bank, (n, e) == (1, 1))
                nc.sync.dma_start(out=out[chans, lo:lo + HALF], in_=y[:])
